import numpy as np
import ml_dtypes


def mxq(x, axis, fmt="e4m3"):
    dtype, down = {"e4m3": (ml_dtypes.float8_e4m3fn, 7), "e5m2": (ml_dtypes.float8_e5m2, 14)}[fmt]
    v = np.moveaxis(np.asarray(x, np.float32).astype(ml_dtypes.bfloat16).astype(np.float64), axis, -1)
    blocks = v.reshape(v.shape[:-1] + (-1, 32))
    amax = np.abs(blocks).max(-1, keepdims=True)
    byte = np.maximum(np.where(amax > 0, np.frexp(amax)[1] - 1 + 127, 0) - down, 1)
    scale = np.exp2(byte - 127.0)
    codes = (blocks / scale).astype(np.float32).astype(dtype).astype(np.float64)
    return np.moveaxis((codes * scale).reshape(v.shape), -1, axis)


WIDE = False


def mx_kscale(k):
    if not WIDE:
        return np.ones(k)
    levels = np.array([10, -10, 5, -5, 0])
    if k % 512:
        return np.exp2(np.random.permutation(np.resize(levels, k // 32))).repeat(32)
    a = np.empty((k // 512, 16))
    for p in range(k // 512):
        a[p, :8] = np.random.permutation(np.resize(levels, 8))
        for g in range(8):
            far = levels[np.abs(levels - a[p, g]) >= 10]
            a[p, g + 8] = far[np.random.randint(len(far))]
    return np.exp2(a.ravel()).repeat(32)


def f64(x):
    return np.asarray(x).astype(np.float64)


def striped(idx):
    return np.tile(idx.reshape(-1, 16).T, (8, 1)).astype(np.uint16)


def unstriped(offs):
    return offs[:16].T.reshape(-1).astype(np.int64)


def relu2(v):
    return np.maximum(v, 0.0) ** 2


K, T, D, S, V, R, N = 1024, 2048, 3, 768, 256, 8, 256


def setup_inputs():
    n = np.random.standard_normal
    s = mx_kscale(K)[:, None]
    return {
        "xT": (n((K, T)) * s).astype(np.float32),
        "w": (n((D, K, N)) / np.sqrt(D * K) / s[None]).astype(np.float32),
        "b": (0.3 * n((N, 1))).astype(np.float32),
        "offs": striped(np.concatenate([R * np.arange(V) + np.random.randint(0, R, V) for _ in range(D)])),
    }


def reference(xT, w, b, offs):
    idx = unstriped(offs)
    xq = mxq(f64(xT)[:, idx], 0, "e4m3")
    wq = mxq(f64(w), 1, "e4m3")
    y = sum(wq[d].T @ xq[:, d * V:(d + 1) * V] for d in range(D))
    y = relu2(y + f64(b))
    return y

@@ -1,0 +1,190 @@
+from contextlib import ExitStack
+
+import concourse.mybir as mybir
+from concourse.masks import make_identity
+
+K, T, D, V, N = 1024, 2048, 3, 256, 256
+S = D * V
+P = 128
+PACK = 4
+PASSES = K // (P * PACK)
+HALVES = N // P
+
+FLOPS = 2 * K * S * N
+
+F32 = mybir.dt.float32
+BF16 = mybir.dt.bfloat16
+U32 = mybir.dt.uint32
+U16 = mybir.dt.uint16
+U8 = mybir.dt.uint8
+FP8X4 = mybir.dt.float8_e4m3fn_x4
+ACT = mybir.ActivationFunctionType
+ALU = mybir.AluOpType
+
+
+def tile_picked_deform_lin_relu2_def_e_kernel(tc, xT, w, b, offs, out):
+    nc = tc.nc
+    with ExitStack() as ctx:
+        hold = ctx.enter_context(tc.tile_pool(name="hold", bufs=1))
+        psum = ctx.enter_context(tc.psum_pool(name="psum", bufs=1))
+
+        offsets = hold.tile([P, S // 16], U16, name="offsets")
+        nc.sync.dma_start(offsets[:], offs)
+
+        x_rows = xT.rearrange("(a p t) n -> a t p n", p=P, t=PACK)
+        w_rows = w.rearrange("d (a p t) m -> d a p t m", p=P, t=PACK)
+        x_raw = {}
+        w_raw = {}
+
+        def load_x(a, t):
+            tile = hold.tile([P, T], F32, name=f"x_raw{a}{t}")
+            nc.sync.dma_start(tile[:], x_rows[a, t])
+            x_raw[a, t] = tile
+
+        def load_w(d, a):
+            tile = hold.tile([P, PACK, N], F32, name=f"w_raw{d}{a}")
+            nc.sync.dma_start(tile[:], w_rows[d, a])
+            w_raw[d, a] = tile
+
+        for t in range(PACK):
+            load_x(0, t)
+        load_w(0, 0)
+        load_x(1, 0)
+        load_x(1, 1)
+        load_x(1, 2)
+        load_w(1, 0)
+        load_x(1, 3)
+        load_w(2, 0)
+        load_w(0, 1)
+        load_w(1, 1)
+        load_w(2, 1)
+
+        bias_rows = hold.tile([P, P], F32, name="bias_rows")
+        nc.gpsimd.memset(bias_rows[:], 0.0)
+        nc.scalar.dma_start(bias_rows[0:HALVES, :], b.rearrange("(h p) o -> h (p o)", p=P))
+        ident = hold.tile([P, P], F32, name="ident")
+        make_identity(nc, ident[:])
+        bias_turned = psum.tile([P, P], F32, name="bias_turned")
+        nc.tensor.transpose(bias_turned[:], bias_rows[:], ident[:])
+        bias = hold.tile([P, HALVES], F32, name="bias")
+        nc.scalar.copy(bias[:], bias_turned[:, 0:HALVES])
+
+        picked = {}
+        x_bf = {}
+        x_codes = {}
+        x_scales = {}
+        w_bf = {}
+        w_codes = {}
+        w_scales = {}
+        for a in range(PASSES):
+            picked[a] = hold.tile([P, PACK, S], F32, name=f"picked{a}")
+            x_bf[a] = hold.tile([P, S, PACK], BF16, name=f"x_bf{a}", align_bytes=64)
+            x_codes[a] = hold.tile([P, S], U32, name=f"x_codes{a}", align_bytes=64)
+            x_scales[a] = hold.tile([P, S], U8, name=f"x_scales{a}", align_bytes=64)
+            for d in range(D):
+                w_bf[d, a] = hold.tile([P, N, PACK], BF16, name=f"w_bf{d}{a}", align_bytes=64)
+                w_codes[d, a] = hold.tile([P, N], U32, name=f"w_codes{d}{a}", align_bytes=64)
+                w_scales[d, a] = hold.tile([P, N], U8, name=f"w_scales{d}{a}", align_bytes=64)
+
+        def gather(a, t, lo, hi):
+            nc.vector.tensor_copy(
+                picked[a][:, t, lo:hi],
+                x_raw[a, t][:].indirect(offsets[:, lo // 16 : hi // 16]),
+            )
+
+        def lay_x(a, lo, hi, t0, t1):
+            nc.scalar.copy(
+                x_bf[a][:, lo:hi, t0:t1],
+                picked[a][:, t0:t1, lo:hi].rearrange("p t n -> p n t"),
+            )
+
+        def lay_w(copy, d, a, lo, hi):
+            copy(
+                w_bf[d, a][:, lo:hi, :],
+                w_raw[d, a][:, :, lo:hi].rearrange("p t m -> p m t"),
+            )
+
+        def quantise(bf, codes, scales, lo, hi):
+            nc.vector.quantize_mx(
+                out=codes[:, lo:hi].bitcast(FP8X4),
+                scales=scales[:, lo:hi],
+                in_=bf[:, lo:hi, :].rearrange("p n t -> p (n t)"),
+            )
+
+        def quantise_x(a, lo, hi):
+            quantise(x_bf[a], x_codes[a], x_scales[a], lo, hi)
+
+        def quantise_w(d, a, lo, hi):
+            quantise(w_bf[d, a], w_codes[d, a], w_scales[d, a], lo, hi)
+
+        acc = [psum.tile([P, V], F32, name=f"acc{h}") for h in range(HALVES)]
+
+        def multiply(d, a, h, start=False, stop=False):
+            m = slice(h * P, (h + 1) * P)
+            v = slice(d * V, (d + 1) * V)
+            nc.tensor.matmul_mx(
+                out=acc[h][:],
+                lhsT=w_codes[d, a][:, m].bitcast(FP8X4),
+                lhsT_scale=w_scales[d, a][:, m],
+                rhs=x_codes[a][:, v].bitcast(FP8X4),
+                rhs_scale=x_scales[a][:, v],
+                start=start,
+                stop=stop,
+            )
+
+        for t in range(PACK):
+            gather(0, t, 0, 512)
+            gather(0, t, 512, S)
+        lay_x(0, 0, 512, 0, PACK)
+        lay_x(0, 512, S, 0, PACK)
+        gather(1, 0, 0, 512)
+        gather(1, 0, 512, S)
+        lay_w(nc.scalar.copy, 0, 0, 0, N)
+        quantise_x(0, 0, 512)
+        quantise_x(0, 512, S)
+        gather(1, 1, 0, 512)
+        gather(1, 1, 512, S)
+        lay_x(1, 0, S, 0, 2)
+        quantise_w(0, 0, 0, N)
+        for h in range(HALVES):
+            multiply(0, 0, h, start=True)
+        gather(1, 2, 0, 512)
+        gather(1, 2, 512, S)
+        lay_w(nc.scalar.copy, 1, 0, 0, N)
+        for d in range(D):
+            gather(1, 3, d * V, (d + 1) * V)
+            lay_x(1, d * V, (d + 1) * V, 2, PACK)
+            if d == 0:
+                quantise_w(1, 0, 0, N)
+                for h in range(HALVES):
+                    multiply(1, 0, h)
+        lay_w(nc.vector.tensor_copy, 2, 0, 0, N)
+        quantise_x(1, 0, V)
+        quantise_w(2, 0, 0, N)
+        for h in range(HALVES):
+            multiply(2, 0, h)
+        lay_w(nc.vector.tensor_copy, 0, 1, 0, N)
+        quantise_x(1, V, 2 * V)
+        quantise_w(0, 1, 0, N)
+        for h in range(HALVES):
+            multiply(0, 1, h)
+        lay_w(nc.scalar.copy, 1, 1, 0, N)
+        quantise_x(1, 2 * V, S)
+        quantise_w(1, 1, 0, N)
+        for h in range(HALVES):
+            multiply(1, 1, h)
+        lay_w(nc.scalar.copy, 2, 1, 0, P)
+        lay_w(nc.vector.tensor_copy, 2, 1, P, N)
+        quantise_w(2, 1, 0, P)
+        multiply(2, 1, 0, stop=True)
+        quantise_w(2, 1, P, N)
+        multiply(2, 1, 1, stop=True)
+
+        relu = [hold.tile([P, V], F32, name=f"relu{h}") for h in range(HALVES)]
+        y = [hold.tile([P, V], F32, name=f"y{h}") for h in range(HALVES)]
+        nc.scalar.activation(relu[0][:], acc[0][:], ACT.Relu, bias=bias[:, 0:1])
+        nc.scalar.activation(y[0][:], relu[0][:], ACT.Square)
+        nc.scalar.dma_start(out[0:P, :], y[0][:])
+        nc.vector.tensor_scalar(relu[1][:], acc[1][:], bias[:, 1:2], 0.0, ALU.add, ALU.max)
+        nc.vector.tensor_tensor(y[1][:], relu[1][:], relu[1][:], ALU.mult)
+        nc.sync.dma_start(out[P:N, :], y[1][:])

@@ -46,14 +46,16 @@ def tile_picked_deform_lin_relu2_def_e_kernel(tc, xT, w, b, offs, out):
             nc.sync.dma_start(tile[:], w_rows[d, a])
             w_raw[d, a] = tile
 
-        for t in range(PACK):
-            load_x(0, t)
+        load_x(0, 0)
+        load_x(0, 1)
+        load_x(0, 2)
+        load_x(0, 3)
         load_w(0, 0)
         load_x(1, 0)
         load_x(1, 1)
         load_x(1, 2)
-        load_w(1, 0)
         load_x(1, 3)
+        load_w(1, 0)
         load_w(2, 0)
         load_w(0, 1)
         load_w(1, 1)
@@ -92,17 +94,17 @@ def tile_picked_deform_lin_relu2_def_e_kernel(tc, xT, w, b, offs, out):
                 x_raw[a, t][:].indirect(offsets[:, lo // 16 : hi // 16]),
             )
 
-        def lay_x(a, lo, hi, t0, t1):
-            nc.scalar.copy(
-                x_bf[a][:, lo:hi, t0:t1],
-                picked[a][:, t0:t1, lo:hi].rearrange("p t n -> p n t"),
+        def lay(copy, dst, src):
+            copy(
+                dst.rearrange("p (c i) t -> p c t i", i=4),
+                src.rearrange("p t (c i) -> p c t i", i=4),
             )
 
+        def lay_x(copy, a, lo, hi, t0, t1):
+            lay(copy, x_bf[a][:, lo:hi, t0:t1], picked[a][:, t0:t1, lo:hi])
+
         def lay_w(copy, d, a, lo, hi):
-            copy(
-                w_bf[d, a][:, lo:hi, :],
-                w_raw[d, a][:, :, lo:hi].rearrange("p t m -> p m t"),
-            )
+            lay(copy, w_bf[d, a][:, lo:hi, :], w_raw[d, a][:, :, lo:hi])
 
         def quantise(bf, codes, scales, lo, hi):
             nc.vector.quantize_mx(
@@ -132,53 +134,61 @@ def tile_picked_deform_lin_relu2_def_e_kernel(tc, xT, w, b, offs, out):
                 stop=stop,
             )
 
-        for t in range(PACK):
+        def on_g(dst, src):
+            nc.gpsimd.tensor_scalar(dst, src, 1.0, 0.0, ALU.mult, ALU.add)
+
+        on_s = nc.scalar.copy
+        on_v = nc.vector.tensor_copy
+        for t in range(3):
             gather(0, t, 0, 512)
             gather(0, t, 512, S)
-        lay_x(0, 0, 512, 0, PACK)
-        lay_x(0, 512, S, 0, PACK)
+        for d in range(D):
+            gather(0, 3, d * V, (d + 1) * V)
+            lay_x(on_s, 0, d * V, (d + 1) * V, 0, PACK)
         gather(1, 0, 0, 512)
+        quantise_x(0, 0, V)
         gather(1, 0, 512, S)
-        lay_w(nc.scalar.copy, 0, 0, 0, N)
-        quantise_x(0, 0, 512)
-        quantise_x(0, 512, S)
+        quantise_x(0, V, 2 * V)
+        lay_w(on_s, 0, 0, 0, N)
         gather(1, 1, 0, 512)
+        quantise_x(0, 2 * V, S)
         gather(1, 1, 512, S)
-        lay_x(1, 0, S, 0, 2)
+        lay_x(on_s, 1, 0, S, 0, 2)
         quantise_w(0, 0, 0, N)
         for h in range(HALVES):
             multiply(0, 0, h, start=True)
         gather(1, 2, 0, 512)
         gather(1, 2, 512, S)
-        lay_w(nc.scalar.copy, 1, 0, 0, N)
         for d in range(D):
             gather(1, 3, d * V, (d + 1) * V)
-            lay_x(1, d * V, (d + 1) * V, 2, PACK)
-            if d == 0:
-                quantise_w(1, 0, 0, N)
-                for h in range(HALVES):
-                    multiply(1, 0, h)
-        lay_w(nc.vector.tensor_copy, 2, 0, 0, N)
+            lay_x(on_s, 1, d * V, (d + 1) * V, 2, PACK)
+        lay_w(on_g, 1, 0, 0, N)
         quantise_x(1, 0, V)
+        lay_w(on_s, 2, 0, 0, N)
+        quantise_x(1, V, 2 * V)
+        quantise_w(1, 0, 0, N)
+        for h in range(HALVES):
+            multiply(1, 0, h)
+        quantise_x(1, 2 * V, S)
+        lay_w(on_s, 0, 1, 0, N)
         quantise_w(2, 0, 0, N)
         for h in range(HALVES):
             multiply(2, 0, h)
-        lay_w(nc.vector.tensor_copy, 0, 1, 0, N)
-        quantise_x(1, V, 2 * V)
+        lay_w(on_v, 1, 1, P, N)
+        lay_w(on_s, 1, 1, 0, P)
         quantise_w(0, 1, 0, N)
         for h in range(HALVES):
             multiply(0, 1, h)
-        lay_w(nc.scalar.copy, 1, 1, 0, N)
-        quantise_x(1, 2 * V, S)
-        quantise_w(1, 1, 0, N)
+        lay_w(on_v, 2, 1, P, N)
+        quantise_w(1, 1, P, N)
+        quantise_w(1, 1, 0, P)
+        lay_w(on_s, 2, 1, 0, P)
         for h in range(HALVES):
             multiply(1, 1, h)
-        lay_w(nc.scalar.copy, 2, 1, 0, P)
-        lay_w(nc.vector.tensor_copy, 2, 1, P, N)
-        quantise_w(2, 1, 0, P)
-        multiply(2, 1, 0, stop=True)
         quantise_w(2, 1, P, N)
         multiply(2, 1, 1, stop=True)
+        quantise_w(2, 1, 0, P)
+        multiply(2, 1, 0, stop=True)
 
         relu = [hold.tile([P, V], F32, name=f"relu{h}") for h in range(HALVES)]
         y = [hold.tile([P, V], F32, name=f"y{h}") for h in range(HALVES)]

@@ -50,11 +50,11 @@ def tile_picked_deform_lin_relu2_def_e_kernel(tc, xT, w, b, offs, out):
         load_x(0, 1)
         load_x(0, 2)
         load_x(0, 3)
-        load_w(0, 0)
         load_x(1, 0)
         load_x(1, 1)
         load_x(1, 2)
         load_x(1, 3)
+        load_w(0, 0)
         load_w(1, 0)
         load_w(2, 0)
         load_w(0, 1)
@@ -149,28 +149,30 @@ def tile_picked_deform_lin_relu2_def_e_kernel(tc, xT, w, b, offs, out):
         quantise_x(0, 0, V)
         gather(1, 0, 512, S)
         quantise_x(0, V, 2 * V)
-        lay_w(on_s, 0, 0, 0, N)
         gather(1, 1, 0, 512)
         quantise_x(0, 2 * V, S)
         gather(1, 1, 512, S)
         lay_x(on_s, 1, 0, S, 0, 2)
-        quantise_w(0, 0, 0, N)
-        for h in range(HALVES):
-            multiply(0, 0, h, start=True)
         gather(1, 2, 0, 512)
         gather(1, 2, 512, S)
         for d in range(D):
             gather(1, 3, d * V, (d + 1) * V)
             lay_x(on_s, 1, d * V, (d + 1) * V, 2, PACK)
-        lay_w(on_g, 1, 0, 0, N)
+        lay_w(on_g, 0, 0, 0, N)
         quantise_x(1, 0, V)
-        lay_w(on_s, 2, 0, 0, N)
+        lay_w(on_s, 1, 0, 0, N)
         quantise_x(1, V, 2 * V)
+        quantise_w(0, 0, 0, N)
+        for h in range(HALVES):
+            multiply(0, 0, h, start=True)
+        quantise_x(1, 2 * V, S)
+        lay_w(on_v, 2, 0, P, N)
+        lay_w(on_s, 2, 0, 0, P)
         quantise_w(1, 0, 0, N)
         for h in range(HALVES):
             multiply(1, 0, h)
-        quantise_x(1, 2 * V, S)
-        lay_w(on_s, 0, 1, 0, N)
+        lay_w(on_v, 0, 1, P, N)
+        lay_w(on_s, 0, 1, 0, P)
         quantise_w(2, 0, 0, N)
         for h in range(HALVES):
             multiply(2, 0, h)
@@ -180,9 +182,8 @@ def tile_picked_deform_lin_relu2_def_e_kernel(tc, xT, w, b, offs, out):
         for h in range(HALVES):
             multiply(0, 1, h)
         lay_w(on_v, 2, 1, P, N)
-        quantise_w(1, 1, P, N)
-        quantise_w(1, 1, 0, P)
         lay_w(on_s, 2, 1, 0, P)
+        quantise_w(1, 1, 0, N)
         for h in range(HALVES):
             multiply(1, 1, h)
         quantise_w(2, 1, P, N)

from contextlib import ExitStack

import concourse.mybir as mybir
from concourse.masks import make_identity

K, T, D, V, N = 1024, 2048, 3, 256, 256
S = D * V
P = 128
PACK = 4
PASSES = K // (P * PACK)
HALVES = N // P

FLOPS = 2 * K * S * N

F32 = mybir.dt.float32
BF16 = mybir.dt.bfloat16
U32 = mybir.dt.uint32
U16 = mybir.dt.uint16
U8 = mybir.dt.uint8
FP8X4 = mybir.dt.float8_e4m3fn_x4
ACT = mybir.ActivationFunctionType
ALU = mybir.AluOpType


def tile_picked_deform_lin_relu2_def_e_kernel(tc, xT, w, b, offs, out):
    nc = tc.nc
    with ExitStack() as ctx:
        hold = ctx.enter_context(tc.tile_pool(name="hold", bufs=1))
        psum = ctx.enter_context(tc.psum_pool(name="psum", bufs=1))

        offsets = hold.tile([P, S // 16], U16, name="offsets")
        nc.sync.dma_start(offsets[:], offs)

        x_rows = xT.rearrange("(a p t) n -> a t p n", p=P, t=PACK)
        w_rows = w.rearrange("d (a p t) m -> d a p t m", p=P, t=PACK)
        x_raw = {}
        w_raw = {}

        def load_x(a, t):
            tile = hold.tile([P, T], F32, name=f"x_raw{a}{t}")
            nc.sync.dma_start(tile[:], x_rows[a, t])
            x_raw[a, t] = tile

        def load_w(d, a):
            tile = hold.tile([P, PACK, N], F32, name=f"w_raw{d}{a}")
            nc.sync.dma_start(tile[:], w_rows[d, a])
            w_raw[d, a] = tile

        load_x(0, 0)
        load_x(0, 1)
        load_x(0, 2)
        load_x(0, 3)
        load_x(1, 0)
        load_x(1, 1)
        load_x(1, 2)
        load_x(1, 3)
        load_w(0, 0)
        load_w(1, 0)
        load_w(2, 0)
        load_w(0, 1)
        load_w(1, 1)
        load_w(2, 1)

        bias_rows = hold.tile([P, P], F32, name="bias_rows")
        nc.gpsimd.memset(bias_rows[:], 0.0)
        nc.scalar.dma_start(bias_rows[0:HALVES, :], b.rearrange("(h p) o -> h (p o)", p=P))
        ident = hold.tile([P, P], F32, name="ident")
        make_identity(nc, ident[:])
        bias_turned = psum.tile([P, P], F32, name="bias_turned")
        nc.tensor.transpose(bias_turned[:], bias_rows[:], ident[:])
        bias = hold.tile([P, HALVES], F32, name="bias")
        nc.scalar.copy(bias[:], bias_turned[:, 0:HALVES])

        picked = {}
        x_bf = {}
        x_codes = {}
        x_scales = {}
        w_bf = {}
        w_codes = {}
        w_scales = {}
        for a in range(PASSES):
            picked[a] = hold.tile([P, PACK, S], F32, name=f"picked{a}")
            x_bf[a] = hold.tile([P, S, PACK], BF16, name=f"x_bf{a}", align_bytes=64)
            x_codes[a] = hold.tile([P, S], U32, name=f"x_codes{a}", align_bytes=64)
            x_scales[a] = hold.tile([P, S], U8, name=f"x_scales{a}", align_bytes=64)
            for d in range(D):
                w_bf[d, a] = hold.tile([P, N, PACK], BF16, name=f"w_bf{d}{a}", align_bytes=64)
                w_codes[d, a] = hold.tile([P, N], U32, name=f"w_codes{d}{a}", align_bytes=64)
                w_scales[d, a] = hold.tile([P, N], U8, name=f"w_scales{d}{a}", align_bytes=64)

        def gather(a, t, lo, hi):
            nc.vector.tensor_copy(
                picked[a][:, t, lo:hi],
                x_raw[a, t][:].indirect(offsets[:, lo // 16 : hi // 16]),
            )

        def lay(copy, dst, src):
            copy(
                dst.rearrange("p (c i) t -> p c t i", i=4),
                src.rearrange("p t (c i) -> p c t i", i=4),
            )

        def lay_x(copy, a, lo, hi, t0, t1):
            lay(copy, x_bf[a][:, lo:hi, t0:t1], picked[a][:, t0:t1, lo:hi])

        def lay_w(copy, d, a, lo, hi):
            lay(copy, w_bf[d, a][:, lo:hi, :], w_raw[d, a][:, :, lo:hi])

        def quantise(bf, codes, scales, lo, hi):
            nc.vector.quantize_mx(
                out=codes[:, lo:hi].bitcast(FP8X4),
                scales=scales[:, lo:hi],
                in_=bf[:, lo:hi, :].rearrange("p n t -> p (n t)"),
            )

        def quantise_x(a, lo, hi):
            quantise(x_bf[a], x_codes[a], x_scales[a], lo, hi)

        def quantise_w(d, a, lo, hi):
            quantise(w_bf[d, a], w_codes[d, a], w_scales[d, a], lo, hi)

        acc = [psum.tile([P, V], F32, name=f"acc{h}") for h in range(HALVES)]

        def multiply(d, a, h, start=False, stop=False):
            m = slice(h * P, (h + 1) * P)
            v = slice(d * V, (d + 1) * V)
            nc.tensor.matmul_mx(
                out=acc[h][:],
                lhsT=w_codes[d, a][:, m].bitcast(FP8X4),
                lhsT_scale=w_scales[d, a][:, m],
                rhs=x_codes[a][:, v].bitcast(FP8X4),
                rhs_scale=x_scales[a][:, v],
                start=start,
                stop=stop,
            )

        def on_g(dst, src):
            nc.gpsimd.tensor_scalar(dst, src, 1.0, 0.0, ALU.mult, ALU.add)

        on_s = nc.scalar.copy
        on_v = nc.vector.tensor_copy
        for t in range(3):
            gather(0, t, 0, 512)
            gather(0, t, 512, S)
        for d in range(D):
            gather(0, 3, d * V, (d + 1) * V)
            lay_x(on_s, 0, d * V, (d + 1) * V, 0, PACK)
        gather(1, 0, 0, 512)
        quantise_x(0, 0, V)
        gather(1, 0, 512, S)
        quantise_x(0, V, 2 * V)
        gather(1, 1, 0, 512)
        quantise_x(0, 2 * V, S)
        gather(1, 1, 512, S)
        lay_x(on_s, 1, 0, S, 0, 2)
        gather(1, 2, 0, 512)
        gather(1, 2, 512, S)
        for d in range(D):
            gather(1, 3, d * V, (d + 1) * V)
            lay_x(on_s, 1, d * V, (d + 1) * V, 2, PACK)
        lay_w(on_g, 0, 0, 0, N)
        quantise_x(1, 0, V)
        lay_w(on_s, 1, 0, 0, N)
        quantise_x(1, V, 2 * V)
        quantise_w(0, 0, 0, N)
        for h in range(HALVES):
            multiply(0, 0, h, start=True)
        quantise_x(1, 2 * V, S)
        lay_w(on_v, 2, 0, P, N)
        lay_w(on_s, 2, 0, 0, P)
        quantise_w(1, 0, 0, N)
        for h in range(HALVES):
            multiply(1, 0, h)
        lay_w(on_v, 0, 1, P, N)
        lay_w(on_s, 0, 1, 0, P)
        quantise_w(2, 0, 0, N)
        for h in range(HALVES):
            multiply(2, 0, h)
        lay_w(on_v, 1, 1, P, N)
        lay_w(on_s, 1, 1, 0, P)
        quantise_w(0, 1, 0, N)
        for h in range(HALVES):
            multiply(0, 1, h)
        lay_w(on_v, 2, 1, P, N)
        lay_w(on_s, 2, 1, 0, P)
        quantise_w(1, 1, 0, N)
        for h in range(HALVES):
            multiply(1, 1, h)
        quantise_w(2, 1, P, N)
        multiply(2, 1, 1, stop=True)
        quantise_w(2, 1, 0, P)
        multiply(2, 1, 0, stop=True)

        relu = [hold.tile([P, V], F32, name=f"relu{h}") for h in range(HALVES)]
        y = [hold.tile([P, V], F32, name=f"y{h}") for h in range(HALVES)]
        nc.scalar.activation(relu[0][:], acc[0][:], ACT.Relu, bias=bias[:, 0:1])
        nc.scalar.activation(y[0][:], relu[0][:], ACT.Square)
        nc.scalar.dma_start(out[0:P, :], y[0][:])
        nc.vector.tensor_scalar(relu[1][:], acc[1][:], bias[:, 1:2], 0.0, ALU.add, ALU.max)
        nc.vector.tensor_tensor(y[1][:], relu[1][:], relu[1][:], ALU.mult)
        nc.sync.dma_start(out[P:N, :], y[1][:])
